import numpy as np
import ml_dtypes


def mxq(x, axis, fmt="e4m3"):
    dtype, down = {"e4m3": (ml_dtypes.float8_e4m3fn, 7), "e5m2": (ml_dtypes.float8_e5m2, 14)}[fmt]
    v = np.moveaxis(np.asarray(x, np.float32).astype(ml_dtypes.bfloat16).astype(np.float64), axis, -1)
    blocks = v.reshape(v.shape[:-1] + (-1, 32))
    amax = np.abs(blocks).max(-1, keepdims=True)
    byte = np.maximum(np.where(amax > 0, np.frexp(amax)[1] - 1 + 127, 0) - down, 1)
    scale = np.exp2(byte - 127.0)
    codes = (blocks / scale).astype(np.float32).astype(dtype).astype(np.float64)
    return np.moveaxis((codes * scale).reshape(v.shape), -1, axis)


WIDE = False


def mx_kscale(k):
    if not WIDE:
        return np.ones(k)
    levels = np.array([10, -10, 5, -5, 0])
    if k % 512:
        return np.exp2(np.random.permutation(np.resize(levels, k // 32))).repeat(32)
    a = np.empty((k // 512, 16))
    for p in range(k // 512):
        a[p, :8] = np.random.permutation(np.resize(levels, 8))
        for g in range(8):
            far = levels[np.abs(levels - a[p, g]) >= 10]
            a[p, g + 8] = far[np.random.randint(len(far))]
    return np.exp2(a.ravel()).repeat(32)


def f64(x):
    return np.asarray(x).astype(np.float64)


def striped(idx):
    return np.tile(idx.reshape(-1, 16).T, (8, 1)).astype(np.uint16)


def unstriped(offs):
    return offs[:16].T.reshape(-1).astype(np.int64)


E2M1 = np.array([0.0, 0.5, 1.0, 1.5, 2.0, 3.0, 4.0, 6.0, -0.0, -0.5, -1.0, -1.5, -2.0, -3.0, -4.0, -6.0])


def pack_weight(w, fmt):
    k, n = w.shape
    w = f64(np.asarray(w, np.float32).astype(ml_dtypes.bfloat16)).reshape(k // 32, 32, n)
    amax = np.abs(w).max(1)
    if fmt == "e4m3":
        byte = np.frexp(amax)[1] - 1 + 127 - 7
    else:
        mant, ex = np.frexp(amax / 6.0)
        byte = np.where(mant > 0.5, ex, ex - 1) + 127
    byte = np.clip(np.where(amax > 0, byte, 1), 1, 254)
    scaled = (w * np.exp2(127.0 - byte)[:, None, :]).reshape(k, n).astype(np.float32)
    by_word = np.ascontiguousarray(scaled.reshape(k // 512, 128, 4, n).transpose(0, 1, 3, 2))
    if fmt == "e4m3":
        words = by_word.astype(ml_dtypes.float8_e4m3fn).view(np.uint8)
    else:
        c = by_word.astype(ml_dtypes.float4_e2m1fn).view(np.uint8) & 0xF
        words = (c[..., 0::2] | (c[..., 1::2] << 4)).reshape(k // 512, 128, 2 * n)
    return np.ascontiguousarray(words), np.ascontiguousarray(byte.astype(np.uint8).reshape(k // 512, 16, n))


def unpack_weight(words, scales, fmt):
    g, _, n = scales.shape
    words = np.ascontiguousarray(words).reshape(g, 128, n, -1)
    if fmt == "e4m3":
        vals = words.view(ml_dtypes.float8_e4m3fn).astype(np.float64)
    else:
        nib = np.empty((g, 128, n, 4), np.uint8)
        nib[..., 0::2] = words & 0xF
        nib[..., 1::2] = words >> 4
        vals = E2M1[nib]
    vals = vals * np.repeat(np.exp2(scales.astype(np.float64) - 127.0), 8, axis=1)[..., None]
    return vals.transpose(0, 1, 3, 2).reshape(g * 512, n)


K, T, E, C, N = 1536, 768, 9, 256, 128
TOP = 3


def by_expert(wq, xq):
    return np.concatenate([wq[e].T @ xq[:, e * C:(e + 1) * C] for e in range(E)], axis=1)


def setup_inputs():
    n = np.random.standard_normal
    s = mx_kscale(K)[:, None]
    deal = np.repeat(np.arange(E), C).reshape(TOP, T)[:, np.random.permutation(T)]
    deal = np.take_along_axis(deal, np.argsort(np.random.rand(TOP, T), axis=0), axis=0)
    for _ in range(8):
        s_, t_ = np.random.permutation(T).reshape(2, -1); r = np.random.randint(TOP, size=T // 2); x, y = deal[r, s_].copy(), deal[r, t_].copy()
        ok = ~((deal[:, s_] == y).any(0) | (deal[:, t_] == x).any(0)); deal[r[ok], s_[ok]] = y[ok]; deal[r[ok], t_[ok]] = x[ok]
    order = np.lexsort((np.random.rand(TOP * T), deal.reshape(-1)))
    slot_token = order % T; pos = np.empty(TOP * T, np.int64); pos[order] = np.arange(TOP * T); pos = pos.reshape(TOP, T)
    g = np.random.uniform(0.5, 1.5, (TOP, T)); g = g / g.sum(0)
    w = [pack_weight(m, "e2m1") for m in n((E + 1, K, N)) / np.sqrt(K) / s[None]]
    return {
        "xT": (n((K, T)) * s).astype(np.float32),
        "w_words": np.stack([m[0] for m in w]),
        "w_scales": np.stack([m[1] for m in w]),
        "b": (0.3 * n((N, E + 1))).astype(np.float32),
        "gate": np.stack([np.tile(r, (N, 1)) for r in g]).astype(np.float32),
        "offs": striped(slot_token),
        "pos1": striped(pos[0]),
        "pos2": striped(pos[1]),
        "pos3": striped(pos[2]),
    }


def reference(xT, w_words, w_scales, b, gate, offs, pos1, pos2, pos3):
    idx = unstriped(offs)
    w = np.stack([unpack_weight(w_words[e], w_scales[e], "e2m1") for e in range(E + 1)])
    wq = w
    xs = mxq(f64(xT), 0, "e4m3")
    ys = (wq[E].T @ xs) + f64(b)[:, E:]
    xq = mxq(f64(xT)[:, idx], 0, "e4m3")
    y = by_expert(w, xq)
    y = y + np.repeat(f64(b)[:, :E], C, axis=1)
    return ys + sum(f64(gate[r]) * y[:, unstriped(p)] for r, p in enumerate((pos1, pos2, pos3)))

@@ -1,0 +1,235 @@
+from contextlib import ExitStack
+
+import concourse.mybir as mybir
+
+K, T, E, C, N = 1536, 768, 9, 256, 128
+TOP = 3
+SLOTS = E * C
+FLOPS = 2 * K * N * (SLOTS + T)
+
+F32 = mybir.dt.float32
+BF16 = mybir.dt.bfloat16
+I32 = mybir.dt.int32
+U32 = mybir.dt.uint32
+U16 = mybir.dt.uint16
+U8 = mybir.dt.uint8
+FP8X4 = mybir.dt.float8_e4m3fn_x4
+FP4X4 = mybir.dt.float4_e2m1fn_x4
+COPY = mybir.ActivationFunctionType.Copy
+IDENTITY = mybir.ActivationFunctionType.Identity
+ADD = mybir.AluOpType.add
+MULT = mybir.AluOpType.mult
+
+P = 128
+PACK = 4
+K_PASS = P * PACK
+PASSES = K // K_PASS
+LAST = PASSES - 1
+LIST_ROWS = 16
+BANK = 512
+SHORT_LIST = 512
+OUT_CHUNK = 256
+ODD = E - 1
+SCALAR_PASSES = (1,)
+FUSED = ((0, 0),)
+
+
+def tile_moe_shr_lin_bias_kernel(tc, xT, w_words, w_scales, b, gate, offs, pos1, pos2, pos3, out):
+    nc = tc.nc
+    with ExitStack() as ctx:
+        lists = ctx.enter_context(tc.tile_pool(name="lists", bufs=1))
+        keep = ctx.enter_context(tc.tile_pool(name="keep", bufs=1))
+        ring = ctx.enter_context(tc.tile_pool(name="ring", bufs=1))
+        psum = ctx.enter_context(tc.psum_pool(name="psum", bufs=1))
+
+        x_rows = [xT[a * K_PASS:(a + 1) * K_PASS, :].rearrange("(p j) t -> p j t", j=PACK) for a in range(PASSES)]
+        half = T // 2
+        raw = {}
+        for c in range(2):
+            raw[0, 0, c] = keep.tile([P, 2, half], F32, name=f"raw_first{c}")
+            nc.sync.dma_start(raw[0, 0, c][:], x_rows[0][:, 0:2, c * half:(c + 1) * half])
+        offs_sb = lists.tile([P, SLOTS // LIST_ROWS], U16, name="offs_sb")
+        nc.sync.dma_start(offs_sb[:], offs)
+        for a in range(PASSES):
+            for h in range(2):
+                if (a, h) != (0, 0):
+                    raw[a, h] = keep.tile([P, 2 * T], F32, name=f"raw{a}{h}")
+                    nc.sync.dma_start(raw[a, h][:].rearrange("p (j t) -> p j t", j=2), x_rows[a][:, 2 * h:2 * h + 2, :])
+
+        matrices = (E + 1) * PASSES
+        w_sb = keep.tile([P, matrices * 2 * N], U8, name="w_sb", align_bytes=64)
+        nc.sync.dma_start(
+            w_sb[:].bitcast(I32).rearrange("p (g c) -> p g c", g=matrices),
+            w_words.rearrange("e a p c -> p (e a) c").bitcast(I32),
+        )
+        ws_sb = keep.tile([P, matrices * N], U8, name="ws_sb", align_bytes=64)
+        nc.vector.memset(ws_sb[:].bitcast(I32), 0)
+        ws_rows = w_scales.rearrange("e a (g r) n -> r g (e a) n", r=4).bitcast(I32)
+        for r in range(4):
+            nc.sync.dma_start(ws_sb[r:P:32, :].bitcast(I32).rearrange("p (g c) -> p g c", g=matrices), ws_rows[r])
+        b_sb = keep.tile([P, E + 1], F32, name="b_sb")
+        nc.sync.dma_start(b_sb[:], b)
+        pos_sb = []
+        for r, pos in enumerate((pos1, pos2, pos3)):
+            pos_sb.append(lists.tile([P, T // LIST_ROWS], U16, name=f"pos_sb{r}"))
+            nc.sync.dma_start(pos_sb[r][:], pos)
+        gate_sb = keep.tile([P, TOP, T], F32, name="gate_sb")
+        nc.sync.dma_start(gate_sb[:], gate.rearrange("r p t -> p r t"))
+
+        pairs = keep.tile([P, PASSES * 2 * 2 * T], BF16, name="pairs")
+
+        def table(a, h, tables):
+            first = (2 * (LAST - a) + h) * 2 * T
+            return pairs[:, first:first + tables * 2 * T]
+
+        def cast(a, h):
+            dst = table(a, h, 1).rearrange("p (t j) -> p t j", j=2)
+            if (a, h) == (0, 0):
+                nc.scalar.activation(dst[:, :half, :], raw[0, 0, 0][:].rearrange("p j t -> p t j"), COPY)
+                nc.vector.tensor_copy(dst[:, half:, :], raw[0, 0, 1][:].rearrange("p j t -> p t j"))
+            else:
+                nc.scalar.activation(dst, raw[a, h][:].rearrange("p (j t) -> p t j", j=2), COPY)
+
+        def list_cols(s0, n):
+            return slice(s0 // LIST_ROWS, (s0 + n) // LIST_ROWS)
+
+        def gather(a, s0, n, tag="got", bufs=2):
+            got = ring.tile([P, 2 * n], U32, name="got", tag=tag, bufs=bufs)
+            step = SHORT_LIST if a == 0 else n
+            for h in range(2):
+                for c in range(0, n, step):
+                    m = min(step, n - c)
+                    window = table(a, h, 1 if m <= SHORT_LIST else 2).bitcast(U32)
+                    nc.vector.tensor_copy(got[:, h * n + c:h * n + c + m], window.indirect(offs_sb[:, list_cols(s0 + c, m)]))
+            return got[:].rearrange("p (h s) -> p h s", h=2)
+
+        def weave(words, woven):
+            nc.scalar.copy(woven.bitcast(U32).rearrange("p (s h) -> p s h", h=2), words.rearrange("p h s -> p s h"))
+
+        def token_words(a):
+            return table(a, 0, 2).bitcast(U32).rearrange("p (h t) -> p h t", h=2)
+
+        def multiply(bank, e, a, codes, scales, start, stop):
+            g = e * PASSES + a
+            nc.tensor.matmul_mx(
+                out=bank,
+                lhsT=w_sb[:, g * 2 * N:(g + 1) * 2 * N].bitcast(FP4X4),
+                lhsT_scale=ws_sb[:, g * N:(g + 1) * N],
+                rhs=codes.bitcast(FP8X4),
+                rhs_scale=scales,
+                start=start,
+                stop=stop,
+            )
+
+        y = keep.tile([P, SLOTS], F32, name="y")
+        slot_banks = [psum.tile([P, min(BANK, SLOTS - s0)], F32, name=f"slot_bank{s0}") for s0 in range(0, SLOTS, BANK)]
+        token_banks = [psum.tile([P, min(BANK, T - t0)], F32, name=f"token_bank{t0}") for t0 in range(0, T, BANK)]
+
+        def expert_product(e, a, codes, scales):
+            j = e % 2
+            multiply(slot_banks[e // 2][:, j * C:(j + 1) * C], e, a, codes, scales,
+                     a == 0 and j == 0, a == LAST and (j == 1 or e == ODD))
+
+        def shared_product(a, codes, scales):
+            for i, bank in enumerate(token_banks):
+                cols = slice(i * BANK, min((i + 1) * BANK, T))
+                multiply(bank[:], E, a, codes[:, cols], scales[:, cols], a == 0, a == LAST)
+
+        def finish(a, s0, n, got, tag="woven", bufs=2):
+            woven = ring.tile([P, PACK * n], BF16, name="woven", tag=tag, bufs=bufs, align_bytes=64)
+            weave(got, woven[:])
+            codes = keep.tile([P, n], U32, name=f"codes{a}_{s0}", align_bytes=64)
+            scales = keep.tile([P, n], U8, name=f"scales{a}_{s0}", align_bytes=64)
+            nc.vector.quantize_mx(out=codes[:].bitcast(FP8X4), scales=scales[:], in_=woven[:])
+            experts = range(s0 // C, (s0 + n) // C)
+            for e in experts:
+                cols = slice(e * C - s0, (e + 1) * C - s0)
+                expert_product(e, a, codes[:, cols], scales[:, cols])
+            return experts
+
+        def evacuate(experts):
+            for e in experts:
+                nc.scalar.activation(y[:, e * C:(e + 1) * C], slot_banks[e // 2][:, (e % 2) * C:(e % 2 + 1) * C], IDENTITY,
+                                     bias=b_sb[:, e:e + 1])
+
+        mixed = [keep.tile([P, PACK * (C + T)], BF16, name=f"mixed{a}", align_bytes=64) for a in range(LAST)]
+
+        def weave_tokens(a):
+            weave(token_words(a), mixed[a][:, PACK * C:])
+
+        def scalar_gather(a):
+            planes = keep.tile([P, PACK, C], F32, name=f"planes{a}")
+            for j in range(PACK):
+                window = raw[a, j // 2][:, (j % 2) * T:(j % 2 + 1) * T]
+                nc.scalar.activation(planes[:, j, :], window.indirect(offs_sb[:, list_cols(ODD * C, C)]), COPY)
+            nc.scalar.activation(mixed[a][:, :PACK * C].rearrange("p (s j) -> p s j", j=PACK),
+                                 planes[:].rearrange("p j s -> p s j"), COPY)
+
+        def finish_mixed(a):
+            codes = keep.tile([P, C + T], U32, name=f"codes_mixed{a}", align_bytes=64)
+            scales = keep.tile([P, C + T], U8, name=f"scales_mixed{a}", align_bytes=64)
+            nc.vector.quantize_mx(out=codes[:].bitcast(FP8X4), scales=scales[:], in_=mixed[a][:])
+            expert_product(ODD, a, codes[:, :C], scales[:, :C])
+            shared_product(a, codes[:, C:], scales[:, C:])
+
+        wide = 4 * C
+        cast(0, 0)
+        cast(0, 1)
+        got00 = gather(0, 0, wide)
+        got01 = gather(0, wide, wide)
+        got02 = gather(0, 2 * wide, C, tag="got_odd", bufs=1)
+        cast(1, 0)
+        cast(1, 1)
+        finish(0, 0, wide, got00)
+        got10 = gather(1, 0, wide)
+        finish(0, wide, wide, got01)
+        weave(got02, mixed[0][:, :PACK * C])
+        weave_tokens(0)
+        finish_mixed(0)
+        got11 = gather(1, wide, wide)
+        cast(2, 0)
+        finish(1, 0, wide, got10)
+        cast(2, 1)
+        got20 = gather(2, 0, wide)
+        finish(1, wide, wide, got11)
+        scalar_gather(1)
+        weave_tokens(1)
+        finish_mixed(1)
+        got21 = gather(2, wide, 2 * C)
+        done = finish(2, 0, wide, got20)
+        tokens_woven = keep.tile([P, PACK * T], BF16, name="tokens_woven", align_bytes=64)
+        weave(token_words(LAST), tokens_woven[:])
+        got22 = gather(2, wide + 2 * C, 2 * C)
+        done2 = finish(2, wide, 2 * C, got21)
+        evacuate(done)
+        got23 = gather(2, 2 * wide, C)
+        done3 = finish(2, wide + 2 * C, 2 * C, got22)
+        evacuate(done2)
+        done4 = finish(2, 2 * wide, C, got23, tag="last", bufs=1)
+        evacuate(done3)
+        evacuate(done4)
+        codes = ring.tile([P, T], U32, name="codes_tokens", tag="last", bufs=1, align_bytes=64)
+        scales = keep.tile([P, T], U8, name="scales_tokens", align_bytes=64)
+        for t0 in range(0, T, BANK):
+            t1 = min(t0 + BANK, T)
+            nc.vector.quantize_mx(out=codes[:, t0:t1].bitcast(FP8X4), scales=scales[:, t0:t1], in_=tokens_woven[:, PACK * t0:PACK * t1])
+        shared_product(LAST, codes, scales)
+
+        for t0 in range(0, T, OUT_CHUNK):
+            cols = slice(t0, t0 + OUT_CHUNK)
+            total = ring.tile([P, OUT_CHUNK], F32, name="total", tag="total", bufs=3)
+            for r in range(TOP):
+                window = y[:].indirect(pos_sb[r][:, list_cols(t0, OUT_CHUNK)])
+                gated = ring.tile([P, OUT_CHUNK], F32, name="gated", tag="gated", bufs=3)
+                if (t0 // OUT_CHUNK, r) in FUSED:
+                    nc.vector.tensor_tensor(gated[:], window, gate_sb[:, r, cols], MULT)
+                else:
+                    picked = ring.tile([P, OUT_CHUNK], F32, name="picked", tag="picked", bufs=9)
+                    nc.scalar.activation(picked[:], window, COPY)
+                    nc.vector.tensor_tensor(gated[:], picked[:], gate_sb[:, r, cols], MULT)
+                if r == 0:
+                    bank = token_banks[t0 // BANK][:, t0 % BANK:t0 % BANK + OUT_CHUNK]
+                    nc.vector.scalar_tensor_tensor(total[:], bank, b_sb[:, E:E + 1], gated[:], ADD, ADD)
+                else:
+                    nc.vector.tensor_tensor(total[:], total[:], gated[:], ADD)
+            nc.sync.dma_start(out[:, cols], total[:])

@@ -30,8 +30,8 @@ BANK = 512
 SHORT_LIST = 512
 OUT_CHUNK = 256
 ODD = E - 1
-SCALAR_PASSES = (1,)
-FUSED = ((0, 0),)
+FIRST_SHARE = 256
+SUM_LAG = 2
 
 
 def tile_moe_shr_lin_bias_kernel(tc, xT, w_words, w_scales, b, gate, offs, pos1, pos2, pos3, out):
@@ -43,18 +43,14 @@ def tile_moe_shr_lin_bias_kernel(tc, xT, w_words, w_scales, b, gate, offs, pos1,
         psum = ctx.enter_context(tc.psum_pool(name="psum", bufs=1))
 
         x_rows = [xT[a * K_PASS:(a + 1) * K_PASS, :].rearrange("(p j) t -> p j t", j=PACK) for a in range(PASSES)]
-        half = T // 2
         raw = {}
-        for c in range(2):
-            raw[0, 0, c] = keep.tile([P, 2, half], F32, name=f"raw_first{c}")
-            nc.sync.dma_start(raw[0, 0, c][:], x_rows[0][:, 0:2, c * half:(c + 1) * half])
         offs_sb = lists.tile([P, SLOTS // LIST_ROWS], U16, name="offs_sb")
-        nc.sync.dma_start(offs_sb[:], offs)
         for a in range(PASSES):
             for h in range(2):
-                if (a, h) != (0, 0):
-                    raw[a, h] = keep.tile([P, 2 * T], F32, name=f"raw{a}{h}")
-                    nc.sync.dma_start(raw[a, h][:].rearrange("p (j t) -> p j t", j=2), x_rows[a][:, 2 * h:2 * h + 2, :])
+                raw[a, h] = keep.tile([P, 2 * T], F32, name=f"raw{a}{h}")
+                nc.sync.dma_start(raw[a, h][:].rearrange("p (j t) -> p j t", j=2), x_rows[a][:, 2 * h:2 * h + 2, :])
+                if (a, h) == (0, 0):
+                    nc.sync.dma_start(offs_sb[:], offs)
 
         matrices = (E + 1) * PASSES
         w_sb = keep.tile([P, matrices * 2 * N], U8, name="w_sb", align_bytes=64)
@@ -84,17 +80,18 @@ def tile_moe_shr_lin_bias_kernel(tc, xT, w_words, w_scales, b, gate, offs, pos1,
 
         def cast(a, h):
             dst = table(a, h, 1).rearrange("p (t j) -> p t j", j=2)
+            src = raw[a, h][:].rearrange("p (j t) -> p t j", j=2)
             if (a, h) == (0, 0):
-                nc.scalar.activation(dst[:, :half, :], raw[0, 0, 0][:].rearrange("p j t -> p t j"), COPY)
-                nc.vector.tensor_copy(dst[:, half:, :], raw[0, 0, 1][:].rearrange("p j t -> p t j"))
+                nc.scalar.activation(dst[:, :FIRST_SHARE, :], src[:, :FIRST_SHARE, :], COPY)
+                nc.vector.tensor_copy(dst[:, FIRST_SHARE:, :], src[:, FIRST_SHARE:, :])
             else:
-                nc.scalar.activation(dst, raw[a, h][:].rearrange("p (j t) -> p t j", j=2), COPY)
+                nc.scalar.activation(dst, src, COPY)
 
         def list_cols(s0, n):
             return slice(s0 // LIST_ROWS, (s0 + n) // LIST_ROWS)
 
         def gather(a, s0, n, tag="got", bufs=2):
-            got = ring.tile([P, 2 * n], U32, name="got", tag=tag, bufs=bufs)
+            got = ring.tile([P, 2 * n], U32, name="got", tag=tag, bufs=bufs, align_bytes=64)
             step = SHORT_LIST if a == 0 else n
             for h in range(2):
                 for c in range(0, n, step):
@@ -122,18 +119,18 @@ def tile_moe_shr_lin_bias_kernel(tc, xT, w_words, w_scales, b, gate, offs, pos1,
             )
 
         y = keep.tile([P, SLOTS], F32, name="y")
-        slot_banks = [psum.tile([P, min(BANK, SLOTS - s0)], F32, name=f"slot_bank{s0}") for s0 in range(0, SLOTS, BANK)]
-        token_banks = [psum.tile([P, min(BANK, T - t0)], F32, name=f"token_bank{t0}") for t0 in range(0, T, BANK)]
+        bank_experts = [(0, 1), (2, 3), (4, 5), (6,), (7,), (8,)]
+        place = {}
+        for group in bank_experts:
+            bank = psum.tile([P, C * len(group)], F32, name=f"slot_bank{group[0]}")
+            for j, e in enumerate(group):
+                place[e] = (bank[:, j * C:(j + 1) * C], j == 0, j == len(group) - 1)
+        token_parts = [(0, OUT_CHUNK), (OUT_CHUNK, T)]
+        token_banks = [psum.tile([P, t1 - t0], F32, name=f"token_bank{t0}") for t0, t1 in token_parts]
 
         def expert_product(e, a, codes, scales):
-            j = e % 2
-            multiply(slot_banks[e // 2][:, j * C:(j + 1) * C], e, a, codes, scales,
-                     a == 0 and j == 0, a == LAST and (j == 1 or e == ODD))
-
-        def shared_product(a, codes, scales):
-            for i, bank in enumerate(token_banks):
-                cols = slice(i * BANK, min((i + 1) * BANK, T))
-                multiply(bank[:], E, a, codes[:, cols], scales[:, cols], a == 0, a == LAST)
+            cols, opens, closes = place[e]
+            multiply(cols, e, a, codes, scales, a == 0 and opens, a == LAST and closes)
 
         def finish(a, s0, n, got, tag="woven", bufs=2):
             woven = ring.tile([P, PACK * n], BF16, name="woven", tag=tag, bufs=bufs, align_bytes=64)
@@ -149,87 +146,130 @@ def tile_moe_shr_lin_bias_kernel(tc, xT, w_words, w_scales, b, gate, offs, pos1,
 
         def evacuate(experts):
             for e in experts:
-                nc.scalar.activation(y[:, e * C:(e + 1) * C], slot_banks[e // 2][:, (e % 2) * C:(e % 2 + 1) * C], IDENTITY,
-                                     bias=b_sb[:, e:e + 1])
+                nc.scalar.activation(y[:, e * C:(e + 1) * C], place[e][0], IDENTITY, bias=b_sb[:, e:e + 1])
 
-        mixed = [keep.tile([P, PACK * (C + T)], BF16, name=f"mixed{a}", align_bytes=64) for a in range(LAST)]
+        def evacuate_vector(experts):
+            for e in experts:
+                nc.vector.tensor_scalar(y[:, e * C:(e + 1) * C], place[e][0], b_sb[:, e:e + 1], None, ADD)
+
+        mixed = keep.tile([P, PACK * (C + T)], BF16, name="mixed", align_bytes=64)
+        odd_woven = keep.tile([P, PACK * C * 1], BF16, name="odd_woven", align_bytes=64)
+        late = [keep.tile([P, PACK * LAST * (t1 - t0)], BF16, name=f"late{t0}", align_bytes=64) for t0, t1 in token_parts]
 
         def weave_tokens(a):
-            weave(token_words(a), mixed[a][:, PACK * C:])
+            if a == 0:
+                weave(token_words(a), mixed[:, PACK * C:])
+            else:
+                for (t0, t1), woven in zip(token_parts, late):
+                    n = PACK * (t1 - t0)
+                    weave(token_words(a)[:, :, t0:t1], woven[:, (a - 1) * n:a * n])
 
-        def scalar_gather(a):
-            planes = keep.tile([P, PACK, C], F32, name=f"planes{a}")
-            for j in range(PACK):
-                window = raw[a, j // 2][:, (j % 2) * T:(j % 2 + 1) * T]
-                nc.scalar.activation(planes[:, j, :], window.indirect(offs_sb[:, list_cols(ODD * C, C)]), COPY)
-            nc.scalar.activation(mixed[a][:, :PACK * C].rearrange("p (s j) -> p s j", j=PACK),
-                                 planes[:].rearrange("p j s -> p s j"), COPY)
+        planes = [keep.tile([P, PACK, C], F32, name=f"planes{a}") for a in range(2)]
 
-        def finish_mixed(a):
-            codes = keep.tile([P, C + T], U32, name=f"codes_mixed{a}", align_bytes=64)
-            scales = keep.tile([P, C + T], U8, name=f"scales_mixed{a}", align_bytes=64)
-            nc.vector.quantize_mx(out=codes[:].bitcast(FP8X4), scales=scales[:], in_=mixed[a][:])
-            expert_product(ODD, a, codes[:, :C], scales[:, :C])
-            shared_product(a, codes[:, C:], scales[:, C:])
+        def scalar_gather(a, h):
+            for j in range(2):
+                window = raw[a, h][:, j * T:(j + 1) * T]
+                nc.scalar.activation(planes[a][:, 2 * h + j, :], window.indirect(offs_sb[:, list_cols(ODD * C, C)]), COPY)
+
+        def scalar_interleave(a):
+            dst = mixed[:, :PACK * C] if a == 0 else odd_woven[:, (a - 1) * PACK * C:a * PACK * C]
+            nc.scalar.activation(dst.rearrange("p (s j) -> p s j", j=PACK),
+                                 planes[a][:].rearrange("p j s -> p s j"), COPY)
+
+        def quantize(woven, codes, name):
+            scales = keep.tile([P, codes.shape[1]], U8, name=f"scales_{name}", align_bytes=64)
+            nc.vector.quantize_mx(out=codes[:].bitcast(FP8X4), scales=scales[:], in_=woven[:])
+            return scales
+
+        def finish_tokens(i):
+            n = token_parts[i][1] - token_parts[i][0]
+            codes = ring.tile([P, LAST * n], U32, name="codes_tokens", tag="got", bufs=2, align_bytes=64)
+            scales = quantize(late[i], codes, f"late{i}")
+            for a in range(1, PASSES):
+                cols = slice((a - 1) * n, a * n)
+                multiply(token_banks[i][:], E, a, codes[:, cols], scales[:, cols], False, a == LAST)
+
+        def finish_odd():
+            codes = keep.tile([P, C * 1], U32, name="codes_odd", align_bytes=64)
+            scales = quantize(odd_woven, codes, "odd")
+            for a in range(1, 2):
+                cols = slice((a - 1) * C, a * C)
+                expert_product(ODD, a, codes[:, cols], scales[:, cols])
+
+        def finish_mixed():
+            codes = keep.tile([P, C + T], U32, name="codes_mixed", align_bytes=64)
+            scales = quantize(mixed, codes, "mixed")
+            expert_product(ODD, 0, codes[:, :C], scales[:, :C])
+            for (t0, t1), bank in zip(token_parts, token_banks):
+                multiply(bank[:], E, 0, codes[:, C + t0:C + t1], scales[:, C + t0:C + t1], True, False)
 
         wide = 4 * C
         cast(0, 0)
+        scalar_gather(0, 0)
         cast(0, 1)
         got00 = gather(0, 0, wide)
         got01 = gather(0, wide, wide)
-        got02 = gather(0, 2 * wide, C, tag="got_odd", bufs=1)
         cast(1, 0)
+        scalar_gather(0, 1)
         cast(1, 1)
+        got10 = gather(1, 0, wide, tag="got_spare", bufs=1)
         finish(0, 0, wide, got00)
-        got10 = gather(1, 0, wide)
         finish(0, wide, wide, got01)
-        weave(got02, mixed[0][:, :PACK * C])
-        weave_tokens(0)
-        finish_mixed(0)
         got11 = gather(1, wide, wide)
+        scalar_interleave(0)
+        weave_tokens(0)
+        finish_mixed()
         cast(2, 0)
         finish(1, 0, wide, got10)
         cast(2, 1)
         got20 = gather(2, 0, wide)
+        scalar_gather(1, 0)
+        scalar_gather(1, 1)
         finish(1, wide, wide, got11)
-        scalar_gather(1)
-        weave_tokens(1)
-        finish_mixed(1)
         got21 = gather(2, wide, 2 * C)
+        scalar_interleave(1)
+        finish_odd()
+        weave_tokens(1)
         done = finish(2, 0, wide, got20)
-        tokens_woven = keep.tile([P, PACK * T], BF16, name="tokens_woven", align_bytes=64)
-        weave(token_words(LAST), tokens_woven[:])
         got22 = gather(2, wide + 2 * C, 2 * C)
+        weave_tokens(2)
         done2 = finish(2, wide, 2 * C, got21)
         evacuate(done)
         got23 = gather(2, 2 * wide, C)
         done3 = finish(2, wide + 2 * C, 2 * C, got22)
         evacuate(done2)
-        done4 = finish(2, 2 * wide, C, got23, tag="last", bufs=1)
+        finish_tokens(0)
+        done4 = finish(2, 2 * wide, C, got23)
+        finish_tokens(1)
         evacuate(done3)
         evacuate(done4)
-        codes = ring.tile([P, T], U32, name="codes_tokens", tag="last", bufs=1, align_bytes=64)
-        scales = keep.tile([P, T], U8, name="scales_tokens", align_bytes=64)
-        for t0 in range(0, T, BANK):
-            t1 = min(t0 + BANK, T)
-            nc.vector.quantize_mx(out=codes[:, t0:t1].bitcast(FP8X4), scales=scales[:, t0:t1], in_=tokens_woven[:, PACK * t0:PACK * t1])
-        shared_product(LAST, codes, scales)
 
-        for t0 in range(0, T, OUT_CHUNK):
+        pieces = [(t0, r) for r in range(TOP) for t0 in range(0, T, OUT_CHUNK)]
+        gated, total = {}, {}
+
+        def gate_product(t0, r):
             cols = slice(t0, t0 + OUT_CHUNK)
-            total = ring.tile([P, OUT_CHUNK], F32, name="total", tag="total", bufs=3)
-            for r in range(TOP):
-                window = y[:].indirect(pos_sb[r][:, list_cols(t0, OUT_CHUNK)])
-                gated = ring.tile([P, OUT_CHUNK], F32, name="gated", tag="gated", bufs=3)
-                if (t0 // OUT_CHUNK, r) in FUSED:
-                    nc.vector.tensor_tensor(gated[:], window, gate_sb[:, r, cols], MULT)
-                else:
-                    picked = ring.tile([P, OUT_CHUNK], F32, name="picked", tag="picked", bufs=9)
-                    nc.scalar.activation(picked[:], window, COPY)
-                    nc.vector.tensor_tensor(gated[:], picked[:], gate_sb[:, r, cols], MULT)
-                if r == 0:
-                    bank = token_banks[t0 // BANK][:, t0 % BANK:t0 % BANK + OUT_CHUNK]
-                    nc.vector.scalar_tensor_tensor(total[:], bank, b_sb[:, E:E + 1], gated[:], ADD, ADD)
-                else:
-                    nc.vector.tensor_tensor(total[:], total[:], gated[:], ADD)
-            nc.sync.dma_start(out[:, cols], total[:])
+            window = y[:].indirect(pos_sb[r][:, list_cols(t0, OUT_CHUNK)])
+            gated[t0, r] = keep.tile([P, OUT_CHUNK], F32, name=f"gated{t0}_{r}")
+            if (t0, r) in pieces[:2]:
+                nc.vector.tensor_tensor(gated[t0, r][:], window, gate_sb[:, r, cols], MULT)
+            else:
+                picked = keep.tile([P, OUT_CHUNK], F32, name=f"picked{t0}_{r}")
+                nc.scalar.activation(picked[:], window, COPY)
+                nc.vector.tensor_tensor(gated[t0, r][:], picked[:], gate_sb[:, r, cols], MULT)
+
+        def add_up(t0, r):
+            if r == 0:
+                total[t0] = keep.tile([P, OUT_CHUNK], F32, name=f"total{t0}")
+                bank = token_banks[0][:] if t0 == 0 else token_banks[1][:, t0 - OUT_CHUNK:t0]
+                nc.vector.scalar_tensor_tensor(total[t0][:], bank, b_sb[:, E:E + 1], gated[t0, r][:], ADD, ADD)
+            else:
+                nc.vector.tensor_tensor(total[t0][:], total[t0][:], gated[t0, r][:], ADD)
+            if r == TOP - 1:
+                nc.sync.dma_start(out[:, t0:t0 + OUT_CHUNK], total[t0][:])
+
+        for i in range(len(pieces) + SUM_LAG):
+            if i < len(pieces):
+                gate_product(*pieces[i])
+            if i >= SUM_LAG:
+                add_up(*pieces[i - SUM_LAG])

@@ -84,14 +84,16 @@ def tile_moe_shr_lin_bias_kernel(tc, xT, w_words, w_scales, b, gate, offs, pos1,
             if (a, h) == (0, 0):
                 nc.scalar.activation(dst[:, :FIRST_SHARE, :], src[:, :FIRST_SHARE, :], COPY)
                 nc.vector.tensor_copy(dst[:, FIRST_SHARE:, :], src[:, FIRST_SHARE:, :])
-            else:
+            elif a == 0:
                 nc.scalar.activation(dst, src, COPY)
+            else:
+                nc.gpsimd.tensor_scalar(dst, src, 1.0, 0.0, MULT, ADD)
 
         def list_cols(s0, n):
             return slice(s0 // LIST_ROWS, (s0 + n) // LIST_ROWS)
 
-        def gather(a, s0, n, tag="got", bufs=2):
-            got = ring.tile([P, 2 * n], U32, name="got", tag=tag, bufs=bufs, align_bytes=64)
+        def gather(a, s0, n, buffer):
+            got = ring.tile([P, 2 * n], U32, name="got", tag=f"got{buffer}", align_bytes=64)
             step = SHORT_LIST if a == 0 else n
             for h in range(2):
                 for c in range(0, n, step):
@@ -132,9 +134,10 @@ def tile_moe_shr_lin_bias_kernel(tc, xT, w_words, w_scales, b, gate, offs, pos1,
             cols, opens, closes = place[e]
             multiply(cols, e, a, codes, scales, a == 0 and opens, a == LAST and closes)
 
-        def finish(a, s0, n, got, tag="woven", bufs=2):
-            woven = ring.tile([P, PACK * n], BF16, name="woven", tag=tag, bufs=bufs, align_bytes=64)
-            weave(got, woven[:])
+        def finish(a, s0, n, got, woven=None):
+            if woven is None:
+                woven = ring.tile([P, PACK * n], BF16, name="woven", tag="woven", bufs=2, align_bytes=64)
+            weave(got, woven[:, :PACK * got.shape[2]])
             codes = keep.tile([P, n], U32, name=f"codes{a}_{s0}", align_bytes=64)
             scales = keep.tile([P, n], U8, name=f"scales{a}_{s0}", align_bytes=64)
             nc.vector.quantize_mx(out=codes[:].bitcast(FP8X4), scales=scales[:], in_=woven[:])
@@ -153,7 +156,7 @@ def tile_moe_shr_lin_bias_kernel(tc, xT, w_words, w_scales, b, gate, offs, pos1,
                 nc.vector.tensor_scalar(y[:, e * C:(e + 1) * C], place[e][0], b_sb[:, e:e + 1], None, ADD)
 
         mixed = keep.tile([P, PACK * (C + T)], BF16, name="mixed", align_bytes=64)
-        odd_woven = keep.tile([P, PACK * C * 1], BF16, name="odd_woven", align_bytes=64)
+        odd_woven = keep.tile([P, PACK * C * 2], BF16, name="odd_woven", align_bytes=64)
         late = [keep.tile([P, PACK * LAST * (t1 - t0)], BF16, name=f"late{t0}", align_bytes=64) for t0, t1 in token_parts]
 
         def weave_tokens(a):
@@ -164,35 +167,35 @@ def tile_moe_shr_lin_bias_kernel(tc, xT, w_words, w_scales, b, gate, offs, pos1,
                     n = PACK * (t1 - t0)
                     weave(token_words(a)[:, :, t0:t1], woven[:, (a - 1) * n:a * n])
 
-        planes = [keep.tile([P, PACK, C], F32, name=f"planes{a}") for a in range(2)]
+        planes = {}
 
-        def scalar_gather(a, h):
+        def scalar_gather(e, a, h):
+            if h == 0:
+                planes[e, a] = ring.tile([P, PACK, C], F32, name="planes", tag="planes", bufs=3)
             for j in range(2):
                 window = raw[a, h][:, j * T:(j + 1) * T]
-                nc.scalar.activation(planes[a][:, 2 * h + j, :], window.indirect(offs_sb[:, list_cols(ODD * C, C)]), COPY)
+                nc.scalar.activation(planes[e, a][:, 2 * h + j, :], window.indirect(offs_sb[:, list_cols(e * C, C)]), COPY)
 
-        def scalar_interleave(a):
-            dst = mixed[:, :PACK * C] if a == 0 else odd_woven[:, (a - 1) * PACK * C:a * PACK * C]
-            nc.scalar.activation(dst.rearrange("p (s j) -> p s j", j=PACK),
-                                 planes[a][:].rearrange("p j s -> p s j"), COPY)
+        def scalar_interleave(e, a, dst):
+            nc.scalar.activation(dst.rearrange("p (s j) -> p s j", j=PACK), planes[e, a][:].rearrange("p j s -> p s j"), COPY)
 
         def quantize(woven, codes, name):
             scales = keep.tile([P, codes.shape[1]], U8, name=f"scales_{name}", align_bytes=64)
             nc.vector.quantize_mx(out=codes[:].bitcast(FP8X4), scales=scales[:], in_=woven[:])
             return scales
 
-        def finish_tokens(i):
+        def finish_tokens(i, buffer):
             n = token_parts[i][1] - token_parts[i][0]
-            codes = ring.tile([P, LAST * n], U32, name="codes_tokens", tag="got", bufs=2, align_bytes=64)
+            codes = ring.tile([P, LAST * n], U32, name="codes_tokens", tag=f"got{buffer}", align_bytes=64)
             scales = quantize(late[i], codes, f"late{i}")
             for a in range(1, PASSES):
                 cols = slice((a - 1) * n, a * n)
                 multiply(token_banks[i][:], E, a, codes[:, cols], scales[:, cols], False, a == LAST)
 
         def finish_odd():
-            codes = keep.tile([P, C * 1], U32, name="codes_odd", align_bytes=64)
+            codes = keep.tile([P, C * 2], U32, name="codes_odd", align_bytes=64)
             scales = quantize(odd_woven, codes, "odd")
-            for a in range(1, 2):
+            for a in range(1, 3):
                 cols = slice((a - 1) * C, a * C)
                 expert_product(ODD, a, codes[:, cols], scales[:, cols])
 
@@ -204,43 +207,52 @@ def tile_moe_shr_lin_bias_kernel(tc, xT, w_words, w_scales, b, gate, offs, pos1,
                 multiply(bank[:], E, 0, codes[:, C + t0:C + t1], scales[:, C + t0:C + t1], True, False)
 
         wide = 4 * C
+        word = PACK * C
         cast(0, 0)
-        scalar_gather(0, 0)
+        scalar_gather(ODD, 0, 0)
         cast(0, 1)
-        got00 = gather(0, 0, wide)
-        got01 = gather(0, wide, wide)
+        got00 = gather(0, 0, wide, 0)
+        got01 = gather(0, wide, wide, 1)
         cast(1, 0)
-        scalar_gather(0, 1)
         cast(1, 1)
-        got10 = gather(1, 0, wide, tag="got_spare", bufs=1)
+        cast(2, 0)
+        cast(2, 1)
+        scalar_gather(ODD, 0, 1)
+        scalar_gather(ODD - 1, 1, 0)
+        scalar_gather(ODD - 1, 1, 1)
+        weave_tokens(0)
+        got10 = gather(1, 0, wide, 2)
         finish(0, 0, wide, got00)
         finish(0, wide, wide, got01)
-        got11 = gather(1, wide, wide)
-        scalar_interleave(0)
-        weave_tokens(0)
+        got11 = gather(1, wide, 3 * C, 0)
+        woven11 = keep.tile([P, PACK * wide], BF16, name="woven11", align_bytes=64)
+        scalar_interleave(ODD - 1, 1, woven11[:, 3 * word:])
+        scalar_interleave(ODD, 0, mixed[:, :word])
         finish_mixed()
-        cast(2, 0)
+        scalar_gather(ODD, 1, 0)
         finish(1, 0, wide, got10)
-        cast(2, 1)
-        got20 = gather(2, 0, wide)
-        scalar_gather(1, 0)
-        scalar_gather(1, 1)
-        finish(1, wide, wide, got11)
-        got21 = gather(2, wide, 2 * C)
-        scalar_interleave(1)
-        finish_odd()
+        got20 = gather(2, 0, wide, 1)
+        scalar_gather(ODD, 1, 1)
+        finish(1, wide, wide, got11, woven11)
+        got21 = gather(2, wide, 2 * C, 0)
         weave_tokens(1)
+        scalar_interleave(ODD, 1, odd_woven[:, :word])
+        scalar_gather(ODD, 2, 0)
         done = finish(2, 0, wide, got20)
-        got22 = gather(2, wide + 2 * C, 2 * C)
+        got22 = gather(2, wide + 2 * C, C, 1)
+        scalar_gather(ODD, 2, 1)
         weave_tokens(2)
         done2 = finish(2, wide, 2 * C, got21)
+        got23 = gather(2, wide + 3 * C, C, 0)
+        scalar_interleave(ODD, 2, odd_woven[:, word:])
+        finish_odd()
         evacuate(done)
-        got23 = gather(2, 2 * wide, C)
-        done3 = finish(2, wide + 2 * C, 2 * C, got22)
+        done3 = finish(2, wide + 2 * C, C, got22)
+        finish_tokens(0, 1)
+        done4 = finish(2, wide + 3 * C, C, got23)
+        finish_tokens(1, 0)
         evacuate(done2)
-        finish_tokens(0)
-        done4 = finish(2, 2 * wide, C, got23)
-        finish_tokens(1)
+        evacuate([ODD])
         evacuate(done3)
         evacuate(done4)
 

@@ -31,6 +31,7 @@ SHORT_LIST = 512
 OUT_CHUNK = 256
 ODD = E - 1
 FIRST_SHARE = 256
+SECOND_SHARE = 192
 SUM_LAG = 2
 
 
@@ -39,7 +40,6 @@ def tile_moe_shr_lin_bias_kernel(tc, xT, w_words, w_scales, b, gate, offs, pos1,
     with ExitStack() as ctx:
         lists = ctx.enter_context(tc.tile_pool(name="lists", bufs=1))
         keep = ctx.enter_context(tc.tile_pool(name="keep", bufs=1))
-        ring = ctx.enter_context(tc.tile_pool(name="ring", bufs=1))
         psum = ctx.enter_context(tc.psum_pool(name="psum", bufs=1))
 
         x_rows = [xT[a * K_PASS:(a + 1) * K_PASS, :].rearrange("(p j) t -> p j t", j=PACK) for a in range(PASSES)]
@@ -47,7 +47,7 @@ def tile_moe_shr_lin_bias_kernel(tc, xT, w_words, w_scales, b, gate, offs, pos1,
         offs_sb = lists.tile([P, SLOTS // LIST_ROWS], U16, name="offs_sb")
         for a in range(PASSES):
             for h in range(2):
-                raw[a, h] = keep.tile([P, 2 * T], F32, name=f"raw{a}{h}")
+                raw[a, h] = keep.tile([P, 2 * T], F32, name="raw", tag="woven1" if (a, h) == (1, 0) else f"raw{a}{h}", align_bytes=64)
                 nc.sync.dma_start(raw[a, h][:].rearrange("p (j t) -> p j t", j=2), x_rows[a][:, 2 * h:2 * h + 2, :])
                 if (a, h) == (0, 0):
                     nc.sync.dma_start(offs_sb[:], offs)
@@ -85,7 +85,8 @@ def tile_moe_shr_lin_bias_kernel(tc, xT, w_words, w_scales, b, gate, offs, pos1,
                 nc.scalar.activation(dst[:, :FIRST_SHARE, :], src[:, :FIRST_SHARE, :], COPY)
                 nc.vector.tensor_copy(dst[:, FIRST_SHARE:, :], src[:, FIRST_SHARE:, :])
             elif a == 0:
-                nc.scalar.activation(dst, src, COPY)
+                nc.scalar.activation(dst[:, :SECOND_SHARE, :], src[:, :SECOND_SHARE, :], COPY)
+                nc.gpsimd.tensor_scalar(dst[:, SECOND_SHARE:, :], src[:, SECOND_SHARE:, :], 1.0, 0.0, MULT, ADD)
             else:
                 nc.gpsimd.tensor_scalar(dst, src, 1.0, 0.0, MULT, ADD)
 
@@ -93,7 +94,7 @@ def tile_moe_shr_lin_bias_kernel(tc, xT, w_words, w_scales, b, gate, offs, pos1,
             return slice(s0 // LIST_ROWS, (s0 + n) // LIST_ROWS)
 
         def gather(a, s0, n, buffer):
-            got = ring.tile([P, 2 * n], U32, name="got", tag=f"got{buffer}", align_bytes=64)
+            got = keep.tile([P, 2 * n], U32, name="got", tag=f"got{buffer}", align_bytes=64)
             step = SHORT_LIST if a == 0 else n
             for h in range(2):
                 for c in range(0, n, step):
@@ -121,7 +122,7 @@ def tile_moe_shr_lin_bias_kernel(tc, xT, w_words, w_scales, b, gate, offs, pos1,
             )
 
         y = keep.tile([P, SLOTS], F32, name="y")
-        bank_experts = [(0, 1), (2, 3), (4, 5), (6,), (7,), (8,)]
+        bank_experts = [(0, 1), (2, 7), (3, 4), (5, 8), (6,)]
         place = {}
         for group in bank_experts:
             bank = psum.tile([P, C * len(group)], F32, name=f"slot_bank{group[0]}")
@@ -134,72 +135,55 @@ def tile_moe_shr_lin_bias_kernel(tc, xT, w_words, w_scales, b, gate, offs, pos1,
             cols, opens, closes = place[e]
             multiply(cols, e, a, codes, scales, a == 0 and opens, a == LAST and closes)
 
-        def finish(a, s0, n, got, woven=None):
-            if woven is None:
-                woven = ring.tile([P, PACK * n], BF16, name="woven", tag="woven", bufs=2, align_bytes=64)
-            weave(got, woven[:, :PACK * got.shape[2]])
-            codes = keep.tile([P, n], U32, name=f"codes{a}_{s0}", align_bytes=64)
-            scales = keep.tile([P, n], U8, name=f"scales{a}_{s0}", align_bytes=64)
-            nc.vector.quantize_mx(out=codes[:].bitcast(FP8X4), scales=scales[:], in_=woven[:])
-            experts = range(s0 // C, (s0 + n) // C)
-            for e in experts:
-                cols = slice(e * C - s0, (e + 1) * C - s0)
+        def woven_tile(n, buffer):
+            return keep.tile([P, PACK * n], BF16, name="woven", tag=f"woven{buffer}", align_bytes=64)
+
+        def finish(a, experts, woven, tag=None):
+            codes = keep.tile([P, C * len(experts)], U32, name="codes", tag=tag or f"codes{a}_{experts[0]}", align_bytes=64)
+            scales = quantize(woven, codes, f"{a}_{experts[0]}")
+            for i, e in enumerate(experts):
+                cols = slice(i * C, (i + 1) * C)
                 expert_product(e, a, codes[:, cols], scales[:, cols])
-            return experts
 
         def evacuate(experts):
             for e in experts:
                 nc.scalar.activation(y[:, e * C:(e + 1) * C], place[e][0], IDENTITY, bias=b_sb[:, e:e + 1])
 
-        def evacuate_vector(experts):
-            for e in experts:
-                nc.vector.tensor_scalar(y[:, e * C:(e + 1) * C], place[e][0], b_sb[:, e:e + 1], None, ADD)
-
-        mixed = keep.tile([P, PACK * (C + T)], BF16, name="mixed", align_bytes=64)
-        odd_woven = keep.tile([P, PACK * C * 2], BF16, name="odd_woven", align_bytes=64)
         late = [keep.tile([P, PACK * LAST * (t1 - t0)], BF16, name=f"late{t0}", align_bytes=64) for t0, t1 in token_parts]
 
         def weave_tokens(a):
-            if a == 0:
-                weave(token_words(a), mixed[:, PACK * C:])
-            else:
-                for (t0, t1), woven in zip(token_parts, late):
-                    n = PACK * (t1 - t0)
-                    weave(token_words(a)[:, :, t0:t1], woven[:, (a - 1) * n:a * n])
+            for (t0, t1), woven in zip(token_parts, late):
+                n = PACK * (t1 - t0)
+                weave(token_words(a)[:, :, t0:t1], woven[:, (a - 1) * n:a * n])
 
         planes = {}
 
         def scalar_gather(e, a, h):
-            if h == 0:
-                planes[e, a] = ring.tile([P, PACK, C], F32, name="planes", tag="planes", bufs=3)
+            if (e, a) not in planes:
+                planes[e, a] = keep.tile([P, PACK, C], F32, name="planes", tag="planes", bufs=4)
             for j in range(2):
                 window = raw[a, h][:, j * T:(j + 1) * T]
                 nc.scalar.activation(planes[e, a][:, 2 * h + j, :], window.indirect(offs_sb[:, list_cols(e * C, C)]), COPY)
 
-        def scalar_interleave(e, a, dst):
-            nc.scalar.activation(dst.rearrange("p (s j) -> p s j", j=PACK), planes[e, a][:].rearrange("p j s -> p s j"), COPY)
+        def interleave(e, a, dst):
+            nc.gpsimd.tensor_scalar(dst.rearrange("p (s j) -> p s j", j=PACK), planes[e, a][:].rearrange("p j s -> p s j"), 1.0, 0.0, MULT, ADD)
 
         def quantize(woven, codes, name):
             scales = keep.tile([P, codes.shape[1]], U8, name=f"scales_{name}", align_bytes=64)
             nc.vector.quantize_mx(out=codes[:].bitcast(FP8X4), scales=scales[:], in_=woven[:])
             return scales
 
-        def finish_tokens(i, buffer):
-            n = token_parts[i][1] - token_parts[i][0]
-            codes = ring.tile([P, LAST * n], U32, name="codes_tokens", tag=f"got{buffer}", align_bytes=64)
-            scales = quantize(late[i], codes, f"late{i}")
-            for a in range(1, PASSES):
-                cols = slice((a - 1) * n, a * n)
-                multiply(token_banks[i][:], E, a, codes[:, cols], scales[:, cols], False, a == LAST)
+        def finish_tokens(buffer):
+            held = keep.tile([P, LAST * T], U32, name="codes_tokens", tag=f"got{buffer}", align_bytes=64)
+            for (t0, t1), woven, bank in zip(token_parts, late, token_banks):
+                n = t1 - t0
+                codes = held[:, LAST * t0:LAST * t1]
+                scales = quantize(woven, codes, f"late{t0}")
+                for a in range(1, PASSES):
+                    cols = slice((a - 1) * n, a * n)
+                    multiply(bank[:], E, a, codes[:, cols], scales[:, cols], False, a == LAST)
 
-        def finish_odd():
-            codes = keep.tile([P, C * 2], U32, name="codes_odd", align_bytes=64)
-            scales = quantize(odd_woven, codes, "odd")
-            for a in range(1, 3):
-                cols = slice((a - 1) * C, a * C)
-                expert_product(ODD, a, codes[:, cols], scales[:, cols])
-
-        def finish_mixed():
+        def finish_mixed(mixed):
             codes = keep.tile([P, C + T], U32, name="codes_mixed", align_bytes=64)
             scales = quantize(mixed, codes, "mixed")
             expert_product(ODD, 0, codes[:, :C], scales[:, :C])
@@ -209,52 +193,68 @@ def tile_moe_shr_lin_bias_kernel(tc, xT, w_words, w_scales, b, gate, offs, pos1,
         wide = 4 * C
         word = PACK * C
         cast(0, 0)
-        scalar_gather(ODD, 0, 0)
+        scalar_gather(7, 0, 0)
         cast(0, 1)
-        got00 = gather(0, 0, wide, 0)
-        got01 = gather(0, wide, wide, 1)
+        got_x0 = gather(0, 0, wide, 0)
+        got_y0 = gather(0, wide, 3 * C, 1)
         cast(1, 0)
         cast(1, 1)
+        scalar_gather(8, 0, 0)
+        scalar_gather(8, 0, 1)
+        scalar_gather(7, 0, 1)
+        scalar_gather(7, 1, 0)
+        scalar_gather(8, 1, 0)
         cast(2, 0)
+        y0 = woven_tile(wide, 1)
+        interleave(7, 0, y0[:, 3 * word:])
         cast(2, 1)
-        scalar_gather(ODD, 0, 1)
-        scalar_gather(ODD - 1, 1, 0)
-        scalar_gather(ODD - 1, 1, 1)
-        weave_tokens(0)
-        got10 = gather(1, 0, wide, 2)
-        finish(0, 0, wide, got00)
-        finish(0, wide, wide, got01)
-        got11 = gather(1, wide, 3 * C, 0)
-        woven11 = keep.tile([P, PACK * wide], BF16, name="woven11", align_bytes=64)
-        scalar_interleave(ODD - 1, 1, woven11[:, 3 * word:])
-        scalar_interleave(ODD, 0, mixed[:, :word])
-        finish_mixed()
-        scalar_gather(ODD, 1, 0)
-        finish(1, 0, wide, got10)
-        got20 = gather(2, 0, wide, 1)
-        scalar_gather(ODD, 1, 1)
-        finish(1, wide, wide, got11, woven11)
-        got21 = gather(2, wide, 2 * C, 0)
+        got_x1 = gather(1, 0, wide, 2)
+        x0 = woven_tile(wide, 0)
+        weave(got_x0, x0[:])
+        scalar_gather(7, 1, 1)
+        scalar_gather(8, 1, 1)
+        finish(0, (0, 1, 2, 3), x0, tag="raw11")
+        weave(got_y0, y0[:, :3 * word])
+        got_y1 = gather(1, wide, 3 * C, 0)
+        finish(0, (4, 5, 6, 7), y0)
+        got_x2 = gather(2, 0, 3 * C, 1)
         weave_tokens(1)
-        scalar_interleave(ODD, 1, odd_woven[:, :word])
-        scalar_gather(ODD, 2, 0)
-        done = finish(2, 0, wide, got20)
-        got22 = gather(2, wide + 2 * C, C, 1)
-        scalar_gather(ODD, 2, 1)
+        mixed = woven_tile(wide, 0)
+        interleave(8, 0, mixed[:, :word])
+        weave(token_words(0), mixed[:, word:])
+        finish_mixed(mixed)
+        lone = woven_tile(C, 3)
+        interleave(8, 1, lone[:])
+        finish(1, (8,), lone)
+        y1 = woven_tile(wide, 1)
+        interleave(7, 1, y1[:, 3 * word:])
+        x1 = woven_tile(wide, 2)
+        weave(got_x1, x1[:])
+        finish(1, (0, 1, 2, 3), x1)
+        got_y2 = gather(2, 3 * C, 3 * C, 2)
+        scalar_gather(7, 2, 0)
+        scalar_gather(7, 2, 1)
+        scalar_gather(8, 2, 0)
+        scalar_gather(8, 2, 1)
+        weave(got_y1, y1[:, :3 * word])
+        finish(1, (4, 5, 6, 7), y1)
+        x2 = woven_tile(wide, 2)
+        interleave(7, 2, x2[:, 3 * word:])
+        weave(got_x2, x2[:, :3 * word])
+        finish(2, (0, 1, 2, 7), x2)
+        got_z2 = gather(2, 6 * C, C, 1)
         weave_tokens(2)
-        done2 = finish(2, wide, 2 * C, got21)
-        got23 = gather(2, wide + 3 * C, C, 0)
-        scalar_interleave(ODD, 2, odd_woven[:, word:])
-        finish_odd()
-        evacuate(done)
-        done3 = finish(2, wide + 2 * C, C, got22)
-        finish_tokens(0, 1)
-        done4 = finish(2, wide + 3 * C, C, got23)
-        finish_tokens(1, 0)
-        evacuate(done2)
-        evacuate([ODD])
-        evacuate(done3)
-        evacuate(done4)
+        y2 = woven_tile(wide, 0)
+        interleave(8, 2, y2[:, 3 * word:])
+        weave(got_y2, y2[:, :3 * word])
+        finish(2, (3, 4), y2[:, :2 * word])
+        finish(2, (5, 8), y2[:, 2 * word:])
+        evacuate((0, 1))
+        z2 = woven_tile(C, 1)
+        weave(got_z2, z2[:])
+        finish(2, (6,), z2)
+        finish_tokens(1)
+        evacuate((2, 7, 3, 4, 5, 8, 6))
 
         pieces = [(t0, r) for r in range(TOP) for t0 in range(0, T, OUT_CHUNK)]
         gated, total = {}, {}

@@ -26,13 +26,16 @@ K_PASS = P * PACK
 PASSES = K // K_PASS
 LAST = PASSES - 1
 LIST_ROWS = 16
-BANK = 512
+SCALE_ROWS = 4
+QUAD = 4 * C
+WOVEN = PACK * C
 SHORT_LIST = 512
 OUT_CHUNK = 256
-ODD = E - 1
-FIRST_SHARE = 256
-SECOND_SHARE = 192
+FIRST_LOADS = ((0, 512), (512, T))
+SCALAR_SHARE = 160
+FUSED_PIECES = 2
 SUM_LAG = 2
+ROW_TILES = 5
 
 
 def tile_moe_shr_lin_bias_kernel(tc, xT, w_words, w_scales, b, gate, offs, pos1, pos2, pos3, out):
@@ -47,8 +50,11 @@ def tile_moe_shr_lin_bias_kernel(tc, xT, w_words, w_scales, b, gate, offs, pos1,
         offs_sb = lists.tile([P, SLOTS // LIST_ROWS], U16, name="offs_sb")
         for a in range(PASSES):
             for h in range(2):
-                raw[a, h] = keep.tile([P, 2 * T], F32, name="raw", tag="woven1" if (a, h) == (1, 0) else f"raw{a}{h}", align_bytes=64)
-                nc.sync.dma_start(raw[a, h][:].rearrange("p (j t) -> p j t", j=2), x_rows[a][:, 2 * h:2 * h + 2, :])
+                tag = "woven1" if (a, h) == (1, 0) else f"raw{a}{h}"
+                raw[a, h] = keep.tile([P, 2 * T], F32, name="raw", tag=tag, align_bytes=64)
+                for t0, t1 in (FIRST_LOADS if (a, h) == (0, 0) else ((0, T),)):
+                    nc.sync.dma_start(raw[a, h][:].rearrange("p (j t) -> p j t", j=2)[:, :, t0:t1],
+                                      x_rows[a][:, 2 * h:2 * h + 2, t0:t1])
                 if (a, h) == (0, 0):
                     nc.sync.dma_start(offs_sb[:], offs)
 
@@ -60,8 +66,8 @@ def tile_moe_shr_lin_bias_kernel(tc, xT, w_words, w_scales, b, gate, offs, pos1,
         )
         ws_sb = keep.tile([P, matrices * N], U8, name="ws_sb", align_bytes=64)
         nc.vector.memset(ws_sb[:].bitcast(I32), 0)
-        ws_rows = w_scales.rearrange("e a (g r) n -> r g (e a) n", r=4).bitcast(I32)
-        for r in range(4):
+        ws_rows = w_scales.rearrange("e a (d r) n -> r d (e a) n", r=SCALE_ROWS).bitcast(I32)
+        for r in range(SCALE_ROWS):
             nc.sync.dma_start(ws_sb[r:P:32, :].bitcast(I32).rearrange("p (g c) -> p g c", g=matrices), ws_rows[r])
         b_sb = keep.tile([P, E + 1], F32, name="b_sb")
         nc.sync.dma_start(b_sb[:], b)
@@ -74,33 +80,39 @@ def tile_moe_shr_lin_bias_kernel(tc, xT, w_words, w_scales, b, gate, offs, pos1,
 
         pairs = keep.tile([P, PASSES * 2 * 2 * T], BF16, name="pairs")
 
-        def table(a, h, tables):
+        def table(a, h, count):
             first = (2 * (LAST - a) + h) * 2 * T
-            return pairs[:, first:first + tables * 2 * T]
+            return pairs[:, first:first + count * 2 * T]
 
-        def cast(a, h):
+        def round_on_gpsimd(dst, src):
+            nc.gpsimd.tensor_scalar(dst, src, 1.0, 0.0, MULT, ADD)
+
+        def round_table(a, h):
             dst = table(a, h, 1).rearrange("p (t j) -> p t j", j=2)
             src = raw[a, h][:].rearrange("p (j t) -> p t j", j=2)
             if (a, h) == (0, 0):
-                nc.scalar.activation(dst[:, :FIRST_SHARE, :], src[:, :FIRST_SHARE, :], COPY)
-                nc.vector.tensor_copy(dst[:, FIRST_SHARE:, :], src[:, FIRST_SHARE:, :])
+                for t0, t1 in FIRST_LOADS:
+                    cut = t0 + (t1 - t0) // 3 // 16 * 16
+                    nc.scalar.activation(dst[:, t0:cut, :], src[:, t0:cut, :], COPY)
+                    nc.vector.tensor_copy(dst[:, cut:t1, :], src[:, cut:t1, :])
             elif a == 0:
-                nc.scalar.activation(dst[:, :SECOND_SHARE, :], src[:, :SECOND_SHARE, :], COPY)
-                nc.gpsimd.tensor_scalar(dst[:, SECOND_SHARE:, :], src[:, SECOND_SHARE:, :], 1.0, 0.0, MULT, ADD)
+                nc.scalar.activation(dst[:, :SCALAR_SHARE, :], src[:, :SCALAR_SHARE, :], COPY)
+                round_on_gpsimd(dst[:, SCALAR_SHARE:, :], src[:, SCALAR_SHARE:, :])
             else:
-                nc.gpsimd.tensor_scalar(dst, src, 1.0, 0.0, MULT, ADD)
+                round_on_gpsimd(dst, src)
 
-        def list_cols(s0, n):
-            return slice(s0 // LIST_ROWS, (s0 + n) // LIST_ROWS)
+        def list_cols(first, count):
+            return slice(first // LIST_ROWS, (first + count) // LIST_ROWS)
 
-        def gather(a, s0, n, buffer):
+        def gather_words(a, e0, e1, buffer):
+            n = (e1 - e0) * C
             got = keep.tile([P, 2 * n], U32, name="got", tag=f"got{buffer}", align_bytes=64)
             step = SHORT_LIST if a == 0 else n
             for h in range(2):
                 for c in range(0, n, step):
                     m = min(step, n - c)
                     window = table(a, h, 1 if m <= SHORT_LIST else 2).bitcast(U32)
-                    nc.vector.tensor_copy(got[:, h * n + c:h * n + c + m], window.indirect(offs_sb[:, list_cols(s0 + c, m)]))
+                    nc.vector.tensor_copy(got[:, h * n + c:h * n + c + m], window.indirect(offs_sb[:, list_cols(e0 * C + c, m)]))
             return got[:].rearrange("p (h s) -> p h s", h=2)
 
         def weave(words, woven):
@@ -109,10 +121,10 @@ def tile_moe_shr_lin_bias_kernel(tc, xT, w_words, w_scales, b, gate, offs, pos1,
         def token_words(a):
             return table(a, 0, 2).bitcast(U32).rearrange("p (h t) -> p h t", h=2)
 
-        def multiply(bank, e, a, codes, scales, start, stop):
+        def multiply(sums, e, a, codes, scales, start, stop):
             g = e * PASSES + a
             nc.tensor.matmul_mx(
-                out=bank,
+                out=sums,
                 lhsT=w_sb[:, g * 2 * N:(g + 1) * 2 * N].bitcast(FP4X4),
                 lhsT_scale=ws_sb[:, g * N:(g + 1) * N],
                 rhs=codes.bitcast(FP8X4),
@@ -122,159 +134,161 @@ def tile_moe_shr_lin_bias_kernel(tc, xT, w_words, w_scales, b, gate, offs, pos1,
             )
 
         y = keep.tile([P, SLOTS], F32, name="y")
-        bank_experts = [(0, 1), (2, 7), (3, 4), (5, 8), (6,)]
-        place = {}
+        bank_experts = [(0, 1), (2,), (3, 4), (5, 8), (6, 7)]
+        place, written = {}, {}
         for group in bank_experts:
             bank = psum.tile([P, C * len(group)], F32, name=f"slot_bank{group[0]}")
-            for j, e in enumerate(group):
-                place[e] = (bank[:, j * C:(j + 1) * C], j == 0, j == len(group) - 1)
+            for i, e in enumerate(group):
+                place[e] = (bank[:, i * C:(i + 1) * C], group)
         token_parts = [(0, OUT_CHUNK), (OUT_CHUNK, T)]
         token_banks = [psum.tile([P, t1 - t0], F32, name=f"token_bank{t0}") for t0, t1 in token_parts]
 
         def expert_product(e, a, codes, scales):
-            cols, opens, closes = place[e]
-            multiply(cols, e, a, codes, scales, a == 0 and opens, a == LAST and closes)
+            sums, group = place[e]
+            issued = written.setdefault(group, [])
+            issued.append((e, a))
+            multiply(sums, e, a, codes, scales, len(issued) == 1, len(issued) == PASSES * len(group))
 
         def woven_tile(n, buffer):
             return keep.tile([P, PACK * n], BF16, name="woven", tag=f"woven{buffer}", align_bytes=64)
-
-        def finish(a, experts, woven, tag=None):
-            codes = keep.tile([P, C * len(experts)], U32, name="codes", tag=tag or f"codes{a}_{experts[0]}", align_bytes=64)
-            scales = quantize(woven, codes, f"{a}_{experts[0]}")
-            for i, e in enumerate(experts):
-                cols = slice(i * C, (i + 1) * C)
-                expert_product(e, a, codes[:, cols], scales[:, cols])
-
-        def evacuate(experts):
-            for e in experts:
-                nc.scalar.activation(y[:, e * C:(e + 1) * C], place[e][0], IDENTITY, bias=b_sb[:, e:e + 1])
-
-        late = [keep.tile([P, PACK * LAST * (t1 - t0)], BF16, name=f"late{t0}", align_bytes=64) for t0, t1 in token_parts]
-
-        def weave_tokens(a):
-            for (t0, t1), woven in zip(token_parts, late):
-                n = PACK * (t1 - t0)
-                weave(token_words(a)[:, :, t0:t1], woven[:, (a - 1) * n:a * n])
-
-        planes = {}
-
-        def scalar_gather(e, a, h):
-            if (e, a) not in planes:
-                planes[e, a] = keep.tile([P, PACK, C], F32, name="planes", tag="planes", bufs=4)
-            for j in range(2):
-                window = raw[a, h][:, j * T:(j + 1) * T]
-                nc.scalar.activation(planes[e, a][:, 2 * h + j, :], window.indirect(offs_sb[:, list_cols(e * C, C)]), COPY)
-
-        def interleave(e, a, dst):
-            nc.gpsimd.tensor_scalar(dst.rearrange("p (s j) -> p s j", j=PACK), planes[e, a][:].rearrange("p j s -> p s j"), 1.0, 0.0, MULT, ADD)
 
         def quantize(woven, codes, name):
             scales = keep.tile([P, codes.shape[1]], U8, name=f"scales_{name}", align_bytes=64)
             nc.vector.quantize_mx(out=codes[:].bitcast(FP8X4), scales=scales[:], in_=woven[:])
             return scales
 
-        def finish_tokens(buffer):
-            held = keep.tile([P, LAST * T], U32, name="codes_tokens", tag=f"got{buffer}", align_bytes=64)
-            for (t0, t1), woven, bank in zip(token_parts, late, token_banks):
-                n = t1 - t0
-                codes = held[:, LAST * t0:LAST * t1]
-                scales = quantize(woven, codes, f"late{t0}")
-                for a in range(1, PASSES):
-                    cols = slice((a - 1) * n, a * n)
-                    multiply(bank[:], E, a, codes[:, cols], scales[:, cols], False, a == LAST)
+        def finish(a, experts, woven, tag=None):
+            codes = keep.tile([P, C * len(experts)], U32, name="codes", tag=tag or f"codes{a}_{experts[0]}", align_bytes=64)
+            scales = quantize(woven, codes, f"{a}_{experts[0]}")
+            for e in experts:
+                i = sorted(experts).index(e)
+                cols = slice(i * C, (i + 1) * C)
+                expert_product(e, a, codes[:, cols], scales[:, cols])
 
-        def finish_mixed(mixed):
-            codes = keep.tile([P, C + T], U32, name="codes_mixed", align_bytes=64)
-            scales = quantize(mixed, codes, "mixed")
-            expert_product(ODD, 0, codes[:, :C], scales[:, :C])
-            for (t0, t1), bank in zip(token_parts, token_banks):
-                multiply(bank[:], E, 0, codes[:, C + t0:C + t1], scales[:, C + t0:C + t1], True, False)
+        late = [keep.tile([P, PACK * LAST * (t1 - t0)], BF16, name=f"late{t0}", align_bytes=64) for t0, t1 in token_parts]
 
-        wide = 4 * C
-        word = PACK * C
-        cast(0, 0)
-        scalar_gather(7, 0, 0)
-        cast(0, 1)
-        got_x0 = gather(0, 0, wide, 0)
-        got_y0 = gather(0, wide, 3 * C, 1)
-        cast(1, 0)
-        cast(1, 1)
-        scalar_gather(8, 0, 0)
-        scalar_gather(8, 0, 1)
-        scalar_gather(7, 0, 1)
-        scalar_gather(7, 1, 0)
-        scalar_gather(8, 1, 0)
-        cast(2, 0)
-        y0 = woven_tile(wide, 1)
-        interleave(7, 0, y0[:, 3 * word:])
-        cast(2, 1)
-        got_x1 = gather(1, 0, wide, 2)
-        x0 = woven_tile(wide, 0)
-        weave(got_x0, x0[:])
-        scalar_gather(7, 1, 1)
-        scalar_gather(8, 1, 1)
-        finish(0, (0, 1, 2, 3), x0, tag="raw11")
-        weave(got_y0, y0[:, :3 * word])
-        got_y1 = gather(1, wide, 3 * C, 0)
-        finish(0, (4, 5, 6, 7), y0)
-        got_x2 = gather(2, 0, 3 * C, 1)
-        weave_tokens(1)
-        mixed = woven_tile(wide, 0)
-        interleave(8, 0, mixed[:, :word])
-        weave(token_words(0), mixed[:, word:])
-        finish_mixed(mixed)
-        lone = woven_tile(C, 3)
-        interleave(8, 1, lone[:])
-        finish(1, (8,), lone)
-        y1 = woven_tile(wide, 1)
-        interleave(7, 1, y1[:, 3 * word:])
-        x1 = woven_tile(wide, 2)
-        weave(got_x1, x1[:])
-        finish(1, (0, 1, 2, 3), x1)
-        got_y2 = gather(2, 3 * C, 3 * C, 2)
-        scalar_gather(7, 2, 0)
-        scalar_gather(7, 2, 1)
-        scalar_gather(8, 2, 0)
-        scalar_gather(8, 2, 1)
-        weave(got_y1, y1[:, :3 * word])
-        finish(1, (4, 5, 6, 7), y1)
-        x2 = woven_tile(wide, 2)
-        interleave(7, 2, x2[:, 3 * word:])
-        weave(got_x2, x2[:, :3 * word])
-        finish(2, (0, 1, 2, 7), x2)
-        got_z2 = gather(2, 6 * C, C, 1)
-        weave_tokens(2)
-        y2 = woven_tile(wide, 0)
-        interleave(8, 2, y2[:, 3 * word:])
-        weave(got_y2, y2[:, :3 * word])
-        finish(2, (3, 4), y2[:, :2 * word])
-        finish(2, (5, 8), y2[:, 2 * word:])
-        evacuate((0, 1))
-        z2 = woven_tile(C, 1)
-        weave(got_z2, z2[:])
-        finish(2, (6,), z2)
-        finish_tokens(1)
-        evacuate((2, 7, 3, 4, 5, 8, 6))
+        def weave_tokens(a, part):
+            t0, t1 = token_parts[part]
+            n = PACK * (t1 - t0)
+            weave(token_words(a)[:, :, t0:t1], late[part][:, (a - 1) * n:a * n])
+
+        rows = {}
+
+        def gather_rows(e, a, h):
+            if (e, a) not in rows:
+                rows[e, a] = keep.tile([P, PACK, C], F32, name="rows", tag="rows", bufs=ROW_TILES)
+            for j in range(2):
+                window = raw[a, h][:, j * T:(j + 1) * T]
+                nc.scalar.activation(rows[e, a][:, 2 * h + j, :], window.indirect(offs_sb[:, list_cols(e * C, C)]), COPY)
+
+        def interleave(e, a, woven):
+            round_on_gpsimd(woven.rearrange("p (s j) -> p s j", j=PACK), rows[e, a][:].rearrange("p j s -> p s j"))
+
+        round_table(0, 0)
+        gather_rows(7, 0, 0)
+        round_table(0, 1)
+        words0_low = gather_words(0, 0, 4, buffer=0)
+        words0_high = gather_words(0, 4, 7, buffer=1)
+        round_table(1, 0)
+        round_table(1, 1)
+        gather_rows(8, 0, 0)
+        gather_rows(8, 0, 1)
+        gather_rows(7, 0, 1)
+        gather_rows(7, 1, 0)
+        gather_rows(8, 1, 0)
+        round_table(2, 0)
+        woven0_high = woven_tile(QUAD, buffer=1)
+        interleave(7, 0, woven0_high[:, 3 * WOVEN:])
+        round_table(2, 1)
+        words1_low = gather_words(1, 0, 4, buffer=2)
+        woven0_low = woven_tile(QUAD, buffer=0)
+        weave(words0_low, woven0_low[:])
+        gather_rows(7, 1, 1)
+        gather_rows(8, 1, 1)
+
+        finish(0, (0, 1, 2, 3), woven0_low, tag="raw11")
+        weave(words0_high, woven0_high[:, :3 * WOVEN])
+        words1_high = gather_words(1, 4, 7, buffer=0)
+        words2_six = keep.tile([P, WOVEN], BF16, name="words2_six")
+        nc.vector.tensor_copy(words2_six[:, :2 * C].bitcast(U32),
+                              table(LAST, 0, 1).bitcast(U32).indirect(offs_sb[:, list_cols(6 * C, C)]))
+        finish(0, (4, 5, 6, 7), woven0_high)
+        words2_low = gather_words(2, 0, 3, buffer=1)
+        for part in range(len(token_parts)):
+            weave_tokens(1, part)
+
+        woven0_rest = woven_tile(C + T, buffer=0)
+        interleave(8, 0, woven0_rest[:, :WOVEN])
+        weave(token_words(0), woven0_rest[:, WOVEN:])
+        codes0_rest = keep.tile([P, C + T], U32, name="codes0_rest", align_bytes=64)
+        scales0_rest = quantize(woven0_rest, codes0_rest, "rest")
+        expert_product(8, 0, codes0_rest[:, :C], scales0_rest[:, :C])
+        for (t0, t1), bank in zip(token_parts, token_banks):
+            multiply(bank[:], E, 0, codes0_rest[:, C + t0:C + t1], scales0_rest[:, C + t0:C + t1], True, False)
+
+        woven1_eight = woven_tile(C, buffer=3)
+        interleave(8, 1, woven1_eight[:])
+        finish(1, (8,), woven1_eight)
+        woven1_high = woven_tile(QUAD, buffer=1)
+        interleave(7, 1, woven1_high[:, 3 * WOVEN:])
+        woven1_low = woven_tile(QUAD, buffer=2)
+        weave(words1_low, woven1_low[:])
+        finish(1, (0, 1, 2, 3), woven1_low)
+        words2_high = gather_words(2, 3, 6, buffer=2)
+        gather_rows(6, 2, 1)
+        round_on_gpsimd(words2_six[:, 2 * C:].rearrange("p (s j) -> p s j", j=2), rows[6, 2][:, 2:, :].rearrange("p j s -> p s j"))
+        for e in (7, 8):
+            for h in range(2):
+                gather_rows(e, 2, h)
+
+        weave_tokens(2, 0)
+        woven2_low = woven_tile(QUAD, buffer=2)
+        interleave(7, 2, woven2_low[:, 3 * WOVEN:])
+        weave(words2_low, woven2_low[:, :3 * WOVEN])
+        finish(2, (0, 1, 2, 7), woven2_low)
+        woven2_six = woven_tile(C, buffer=3)
+        weave(words2_six[:].bitcast(U32).rearrange("p (h s) -> p h s", h=2), woven2_six[:])
+        finish(2, (6,), woven2_six)
+        weave(words1_high, woven1_high[:, :3 * WOVEN])
+        finish(1, (6, 7, 4, 5), woven1_high)
+        woven2_high = woven_tile(QUAD, buffer=0)
+        interleave(8, 2, woven2_high[:, 3 * WOVEN:])
+        weave(words2_high, woven2_high[:, :3 * WOVEN])
+        finish(2, (3, 4), woven2_high[:, :2 * WOVEN])
+        finish(2, (5, 8), woven2_high[:, 2 * WOVEN:])
+        weave_tokens(2, 1)
+
+        codes_late = keep.tile([P, LAST * T], U32, name="codes_late", tag="got2", align_bytes=64)
+        for (t0, t1), woven, bank in zip(token_parts, late, token_banks):
+            n = t1 - t0
+            codes = codes_late[:, LAST * t0:LAST * t1]
+            scales = quantize(woven, codes, f"late{t0}")
+            for a in range(1, PASSES):
+                cols = slice((a - 1) * n, a * n)
+                multiply(bank[:], E, a, codes[:, cols], scales[:, cols], False, a == LAST)
+
+        for e in (0, 1, 2, 6, 7, 3, 4, 5, 8):
+            nc.scalar.activation(y[:, e * C:(e + 1) * C], place[e][0], IDENTITY, bias=b_sb[:, e:e + 1])
 
         pieces = [(t0, r) for r in range(TOP) for t0 in range(0, T, OUT_CHUNK)]
         gated, total = {}, {}
 
         def gate_product(t0, r):
             cols = slice(t0, t0 + OUT_CHUNK)
-            window = y[:].indirect(pos_sb[r][:, list_cols(t0, OUT_CHUNK)])
+            looked_up = y[:].indirect(pos_sb[r][:, list_cols(t0, OUT_CHUNK)])
             gated[t0, r] = keep.tile([P, OUT_CHUNK], F32, name=f"gated{t0}_{r}")
-            if (t0, r) in pieces[:2]:
-                nc.vector.tensor_tensor(gated[t0, r][:], window, gate_sb[:, r, cols], MULT)
+            if (t0, r) in pieces[:FUSED_PIECES]:
+                nc.vector.tensor_tensor(gated[t0, r][:], looked_up, gate_sb[:, r, cols], MULT)
             else:
                 picked = keep.tile([P, OUT_CHUNK], F32, name=f"picked{t0}_{r}")
-                nc.scalar.activation(picked[:], window, COPY)
+                nc.scalar.activation(picked[:], looked_up, COPY)
                 nc.vector.tensor_tensor(gated[t0, r][:], picked[:], gate_sb[:, r, cols], MULT)
 
         def add_up(t0, r):
             if r == 0:
                 total[t0] = keep.tile([P, OUT_CHUNK], F32, name=f"total{t0}")
-                bank = token_banks[0][:] if t0 == 0 else token_banks[1][:, t0 - OUT_CHUNK:t0]
-                nc.vector.scalar_tensor_tensor(total[t0][:], bank, b_sb[:, E:E + 1], gated[t0, r][:], ADD, ADD)
+                sums = token_banks[0][:] if t0 == 0 else token_banks[1][:, t0 - OUT_CHUNK:t0]
+                nc.vector.scalar_tensor_tensor(total[t0][:], sums, b_sb[:, E:E + 1], gated[t0, r][:], ADD, ADD)
             else:
                 nc.vector.tensor_tensor(total[t0][:], total[t0][:], gated[t0, r][:], ADD)
             if r == TOP - 1:

from contextlib import ExitStack

import concourse.mybir as mybir

K, T, E, C, N = 1536, 768, 9, 256, 128
TOP = 3
SLOTS = E * C
FLOPS = 2 * K * N * (SLOTS + T)

F32 = mybir.dt.float32
BF16 = mybir.dt.bfloat16
I32 = mybir.dt.int32
U32 = mybir.dt.uint32
U16 = mybir.dt.uint16
U8 = mybir.dt.uint8
FP8X4 = mybir.dt.float8_e4m3fn_x4
FP4X4 = mybir.dt.float4_e2m1fn_x4
COPY = mybir.ActivationFunctionType.Copy
IDENTITY = mybir.ActivationFunctionType.Identity
ADD = mybir.AluOpType.add
MULT = mybir.AluOpType.mult

P = 128
PACK = 4
K_PASS = P * PACK
PASSES = K // K_PASS
LAST = PASSES - 1
LIST_ROWS = 16
SCALE_ROWS = 4
QUAD = 4 * C
WOVEN = PACK * C
SHORT_LIST = 512
OUT_CHUNK = 256
FIRST_LOADS = ((0, 512), (512, T))
SCALAR_SHARE = 160
FUSED_PIECES = 2
SUM_LAG = 2
ROW_TILES = 5


def tile_moe_shr_lin_bias_kernel(tc, xT, w_words, w_scales, b, gate, offs, pos1, pos2, pos3, out):
    nc = tc.nc
    with ExitStack() as ctx:
        lists = ctx.enter_context(tc.tile_pool(name="lists", bufs=1))
        keep = ctx.enter_context(tc.tile_pool(name="keep", bufs=1))
        psum = ctx.enter_context(tc.psum_pool(name="psum", bufs=1))

        x_rows = [xT[a * K_PASS:(a + 1) * K_PASS, :].rearrange("(p j) t -> p j t", j=PACK) for a in range(PASSES)]
        raw = {}
        offs_sb = lists.tile([P, SLOTS // LIST_ROWS], U16, name="offs_sb")
        for a in range(PASSES):
            for h in range(2):
                tag = "woven1" if (a, h) == (1, 0) else f"raw{a}{h}"
                raw[a, h] = keep.tile([P, 2 * T], F32, name="raw", tag=tag, align_bytes=64)
                for t0, t1 in (FIRST_LOADS if (a, h) == (0, 0) else ((0, T),)):
                    nc.sync.dma_start(raw[a, h][:].rearrange("p (j t) -> p j t", j=2)[:, :, t0:t1],
                                      x_rows[a][:, 2 * h:2 * h + 2, t0:t1])
                if (a, h) == (0, 0):
                    nc.sync.dma_start(offs_sb[:], offs)

        matrices = (E + 1) * PASSES
        w_sb = keep.tile([P, matrices * 2 * N], U8, name="w_sb", align_bytes=64)
        nc.sync.dma_start(
            w_sb[:].bitcast(I32).rearrange("p (g c) -> p g c", g=matrices),
            w_words.rearrange("e a p c -> p (e a) c").bitcast(I32),
        )
        ws_sb = keep.tile([P, matrices * N], U8, name="ws_sb", align_bytes=64)
        nc.vector.memset(ws_sb[:].bitcast(I32), 0)
        ws_rows = w_scales.rearrange("e a (d r) n -> r d (e a) n", r=SCALE_ROWS).bitcast(I32)
        for r in range(SCALE_ROWS):
            nc.sync.dma_start(ws_sb[r:P:32, :].bitcast(I32).rearrange("p (g c) -> p g c", g=matrices), ws_rows[r])
        b_sb = keep.tile([P, E + 1], F32, name="b_sb")
        nc.sync.dma_start(b_sb[:], b)
        pos_sb = []
        for r, pos in enumerate((pos1, pos2, pos3)):
            pos_sb.append(lists.tile([P, T // LIST_ROWS], U16, name=f"pos_sb{r}"))
            nc.sync.dma_start(pos_sb[r][:], pos)
        gate_sb = keep.tile([P, TOP, T], F32, name="gate_sb")
        nc.sync.dma_start(gate_sb[:], gate.rearrange("r p t -> p r t"))

        pairs = keep.tile([P, PASSES * 2 * 2 * T], BF16, name="pairs")

        def table(a, h, count):
            first = (2 * (LAST - a) + h) * 2 * T
            return pairs[:, first:first + count * 2 * T]

        def round_on_gpsimd(dst, src):
            nc.gpsimd.tensor_scalar(dst, src, 1.0, 0.0, MULT, ADD)

        def round_table(a, h):
            dst = table(a, h, 1).rearrange("p (t j) -> p t j", j=2)
            src = raw[a, h][:].rearrange("p (j t) -> p t j", j=2)
            if (a, h) == (0, 0):
                for t0, t1 in FIRST_LOADS:
                    cut = t0 + (t1 - t0) // 3 // 16 * 16
                    nc.scalar.activation(dst[:, t0:cut, :], src[:, t0:cut, :], COPY)
                    nc.vector.tensor_copy(dst[:, cut:t1, :], src[:, cut:t1, :])
            elif a == 0:
                nc.scalar.activation(dst[:, :SCALAR_SHARE, :], src[:, :SCALAR_SHARE, :], COPY)
                round_on_gpsimd(dst[:, SCALAR_SHARE:, :], src[:, SCALAR_SHARE:, :])
            else:
                round_on_gpsimd(dst, src)

        def list_cols(first, count):
            return slice(first // LIST_ROWS, (first + count) // LIST_ROWS)

        def gather_words(a, e0, e1, buffer):
            n = (e1 - e0) * C
            got = keep.tile([P, 2 * n], U32, name="got", tag=f"got{buffer}", align_bytes=64)
            step = SHORT_LIST if a == 0 else n
            for h in range(2):
                for c in range(0, n, step):
                    m = min(step, n - c)
                    window = table(a, h, 1 if m <= SHORT_LIST else 2).bitcast(U32)
                    nc.vector.tensor_copy(got[:, h * n + c:h * n + c + m], window.indirect(offs_sb[:, list_cols(e0 * C + c, m)]))
            return got[:].rearrange("p (h s) -> p h s", h=2)

        def weave(words, woven):
            nc.scalar.copy(woven.bitcast(U32).rearrange("p (s h) -> p s h", h=2), words.rearrange("p h s -> p s h"))

        def token_words(a):
            return table(a, 0, 2).bitcast(U32).rearrange("p (h t) -> p h t", h=2)

        def multiply(sums, e, a, codes, scales, start, stop):
            g = e * PASSES + a
            nc.tensor.matmul_mx(
                out=sums,
                lhsT=w_sb[:, g * 2 * N:(g + 1) * 2 * N].bitcast(FP4X4),
                lhsT_scale=ws_sb[:, g * N:(g + 1) * N],
                rhs=codes.bitcast(FP8X4),
                rhs_scale=scales,
                start=start,
                stop=stop,
            )

        y = keep.tile([P, SLOTS], F32, name="y")
        bank_experts = [(0, 1), (2,), (3, 4), (5, 8), (6, 7)]
        place, written = {}, {}
        for group in bank_experts:
            bank = psum.tile([P, C * len(group)], F32, name=f"slot_bank{group[0]}")
            for i, e in enumerate(group):
                place[e] = (bank[:, i * C:(i + 1) * C], group)
        token_parts = [(0, OUT_CHUNK), (OUT_CHUNK, T)]
        token_banks = [psum.tile([P, t1 - t0], F32, name=f"token_bank{t0}") for t0, t1 in token_parts]

        def expert_product(e, a, codes, scales):
            sums, group = place[e]
            issued = written.setdefault(group, [])
            issued.append((e, a))
            multiply(sums, e, a, codes, scales, len(issued) == 1, len(issued) == PASSES * len(group))

        def woven_tile(n, buffer):
            return keep.tile([P, PACK * n], BF16, name="woven", tag=f"woven{buffer}", align_bytes=64)

        def quantize(woven, codes, name):
            scales = keep.tile([P, codes.shape[1]], U8, name=f"scales_{name}", align_bytes=64)
            nc.vector.quantize_mx(out=codes[:].bitcast(FP8X4), scales=scales[:], in_=woven[:])
            return scales

        def finish(a, experts, woven, tag=None):
            codes = keep.tile([P, C * len(experts)], U32, name="codes", tag=tag or f"codes{a}_{experts[0]}", align_bytes=64)
            scales = quantize(woven, codes, f"{a}_{experts[0]}")
            for e in experts:
                i = sorted(experts).index(e)
                cols = slice(i * C, (i + 1) * C)
                expert_product(e, a, codes[:, cols], scales[:, cols])

        late = [keep.tile([P, PACK * LAST * (t1 - t0)], BF16, name=f"late{t0}", align_bytes=64) for t0, t1 in token_parts]

        def weave_tokens(a, part):
            t0, t1 = token_parts[part]
            n = PACK * (t1 - t0)
            weave(token_words(a)[:, :, t0:t1], late[part][:, (a - 1) * n:a * n])

        rows = {}

        def gather_rows(e, a, h):
            if (e, a) not in rows:
                rows[e, a] = keep.tile([P, PACK, C], F32, name="rows", tag="rows", bufs=ROW_TILES)
            for j in range(2):
                window = raw[a, h][:, j * T:(j + 1) * T]
                nc.scalar.activation(rows[e, a][:, 2 * h + j, :], window.indirect(offs_sb[:, list_cols(e * C, C)]), COPY)

        def interleave(e, a, woven):
            round_on_gpsimd(woven.rearrange("p (s j) -> p s j", j=PACK), rows[e, a][:].rearrange("p j s -> p s j"))

        round_table(0, 0)
        gather_rows(7, 0, 0)
        round_table(0, 1)
        words0_low = gather_words(0, 0, 4, buffer=0)
        words0_high = gather_words(0, 4, 7, buffer=1)
        round_table(1, 0)
        round_table(1, 1)
        gather_rows(8, 0, 0)
        gather_rows(8, 0, 1)
        gather_rows(7, 0, 1)
        gather_rows(7, 1, 0)
        gather_rows(8, 1, 0)
        round_table(2, 0)
        woven0_high = woven_tile(QUAD, buffer=1)
        interleave(7, 0, woven0_high[:, 3 * WOVEN:])
        round_table(2, 1)
        words1_low = gather_words(1, 0, 4, buffer=2)
        woven0_low = woven_tile(QUAD, buffer=0)
        weave(words0_low, woven0_low[:])
        gather_rows(7, 1, 1)
        gather_rows(8, 1, 1)

        finish(0, (0, 1, 2, 3), woven0_low, tag="raw11")
        weave(words0_high, woven0_high[:, :3 * WOVEN])
        words1_high = gather_words(1, 4, 7, buffer=0)
        words2_six = keep.tile([P, WOVEN], BF16, name="words2_six")
        nc.vector.tensor_copy(words2_six[:, :2 * C].bitcast(U32),
                              table(LAST, 0, 1).bitcast(U32).indirect(offs_sb[:, list_cols(6 * C, C)]))
        finish(0, (4, 5, 6, 7), woven0_high)
        words2_low = gather_words(2, 0, 3, buffer=1)
        for part in range(len(token_parts)):
            weave_tokens(1, part)

        woven0_rest = woven_tile(C + T, buffer=0)
        interleave(8, 0, woven0_rest[:, :WOVEN])
        weave(token_words(0), woven0_rest[:, WOVEN:])
        codes0_rest = keep.tile([P, C + T], U32, name="codes0_rest", align_bytes=64)
        scales0_rest = quantize(woven0_rest, codes0_rest, "rest")
        expert_product(8, 0, codes0_rest[:, :C], scales0_rest[:, :C])
        for (t0, t1), bank in zip(token_parts, token_banks):
            multiply(bank[:], E, 0, codes0_rest[:, C + t0:C + t1], scales0_rest[:, C + t0:C + t1], True, False)

        woven1_eight = woven_tile(C, buffer=3)
        interleave(8, 1, woven1_eight[:])
        finish(1, (8,), woven1_eight)
        woven1_high = woven_tile(QUAD, buffer=1)
        interleave(7, 1, woven1_high[:, 3 * WOVEN:])
        woven1_low = woven_tile(QUAD, buffer=2)
        weave(words1_low, woven1_low[:])
        finish(1, (0, 1, 2, 3), woven1_low)
        words2_high = gather_words(2, 3, 6, buffer=2)
        gather_rows(6, 2, 1)
        round_on_gpsimd(words2_six[:, 2 * C:].rearrange("p (s j) -> p s j", j=2), rows[6, 2][:, 2:, :].rearrange("p j s -> p s j"))
        for e in (7, 8):
            for h in range(2):
                gather_rows(e, 2, h)

        weave_tokens(2, 0)
        woven2_low = woven_tile(QUAD, buffer=2)
        interleave(7, 2, woven2_low[:, 3 * WOVEN:])
        weave(words2_low, woven2_low[:, :3 * WOVEN])
        finish(2, (0, 1, 2, 7), woven2_low)
        woven2_six = woven_tile(C, buffer=3)
        weave(words2_six[:].bitcast(U32).rearrange("p (h s) -> p h s", h=2), woven2_six[:])
        finish(2, (6,), woven2_six)
        weave(words1_high, woven1_high[:, :3 * WOVEN])
        finish(1, (6, 7, 4, 5), woven1_high)
        woven2_high = woven_tile(QUAD, buffer=0)
        interleave(8, 2, woven2_high[:, 3 * WOVEN:])
        weave(words2_high, woven2_high[:, :3 * WOVEN])
        finish(2, (3, 4), woven2_high[:, :2 * WOVEN])
        finish(2, (5, 8), woven2_high[:, 2 * WOVEN:])
        weave_tokens(2, 1)

        codes_late = keep.tile([P, LAST * T], U32, name="codes_late", tag="got2", align_bytes=64)
        for (t0, t1), woven, bank in zip(token_parts, late, token_banks):
            n = t1 - t0
            codes = codes_late[:, LAST * t0:LAST * t1]
            scales = quantize(woven, codes, f"late{t0}")
            for a in range(1, PASSES):
                cols = slice((a - 1) * n, a * n)
                multiply(bank[:], E, a, codes[:, cols], scales[:, cols], False, a == LAST)

        for e in (0, 1, 2, 6, 7, 3, 4, 5, 8):
            nc.scalar.activation(y[:, e * C:(e + 1) * C], place[e][0], IDENTITY, bias=b_sb[:, e:e + 1])

        pieces = [(t0, r) for r in range(TOP) for t0 in range(0, T, OUT_CHUNK)]
        gated, total = {}, {}

        def gate_product(t0, r):
            cols = slice(t0, t0 + OUT_CHUNK)
            looked_up = y[:].indirect(pos_sb[r][:, list_cols(t0, OUT_CHUNK)])
            gated[t0, r] = keep.tile([P, OUT_CHUNK], F32, name=f"gated{t0}_{r}")
            if (t0, r) in pieces[:FUSED_PIECES]:
                nc.vector.tensor_tensor(gated[t0, r][:], looked_up, gate_sb[:, r, cols], MULT)
            else:
                picked = keep.tile([P, OUT_CHUNK], F32, name=f"picked{t0}_{r}")
                nc.scalar.activation(picked[:], looked_up, COPY)
                nc.vector.tensor_tensor(gated[t0, r][:], picked[:], gate_sb[:, r, cols], MULT)

        def add_up(t0, r):
            if r == 0:
                total[t0] = keep.tile([P, OUT_CHUNK], F32, name=f"total{t0}")
                sums = token_banks[0][:] if t0 == 0 else token_banks[1][:, t0 - OUT_CHUNK:t0]
                nc.vector.scalar_tensor_tensor(total[t0][:], sums, b_sb[:, E:E + 1], gated[t0, r][:], ADD, ADD)
            else:
                nc.vector.tensor_tensor(total[t0][:], total[t0][:], gated[t0, r][:], ADD)
            if r == TOP - 1:
                nc.sync.dma_start(out[:, t0:t0 + OUT_CHUNK], total[t0][:])

        for i in range(len(pieces) + SUM_LAG):
            if i < len(pieces):
                gate_product(*pieces[i])
            if i >= SUM_LAG:
                add_up(*pieces[i - SUM_LAG])
